import numpy as np
import ml_dtypes


def mxq(x, axis, fmt="e4m3"):
    dtype, down = {"e4m3": (ml_dtypes.float8_e4m3fn, 7), "e5m2": (ml_dtypes.float8_e5m2, 14)}[fmt]
    v = np.moveaxis(np.asarray(x, np.float32).astype(ml_dtypes.bfloat16).astype(np.float64), axis, -1)
    blocks = v.reshape(v.shape[:-1] + (-1, 32))
    amax = np.abs(blocks).max(-1, keepdims=True)
    byte = np.maximum(np.where(amax > 0, np.frexp(amax)[1] - 1 + 127, 0) - down, 1)
    scale = np.exp2(byte - 127.0)
    codes = (blocks / scale).astype(np.float32).astype(dtype).astype(np.float64)
    return np.moveaxis((codes * scale).reshape(v.shape), -1, axis)


WIDE = False


def mx_kscale(k):
    if not WIDE:
        return np.ones(k)
    levels = np.array([10, -10, 5, -5, 0])
    if k % 512:
        return np.exp2(np.random.permutation(np.resize(levels, k // 32))).repeat(32)
    a = np.empty((k // 512, 16))
    for p in range(k // 512):
        a[p, :8] = np.random.permutation(np.resize(levels, 8))
        for g in range(8):
            far = levels[np.abs(levels - a[p, g]) >= 10]
            a[p, g + 8] = far[np.random.randint(len(far))]
    return np.exp2(a.ravel()).repeat(32)


def f64(x):
    return np.asarray(x).astype(np.float64)


def striped(idx):
    return np.tile(idx.reshape(-1, 16).T, (8, 1)).astype(np.uint16)


def unstriped(offs):
    return offs[:16].T.reshape(-1).astype(np.int64)


E2M1 = np.array([0.0, 0.5, 1.0, 1.5, 2.0, 3.0, 4.0, 6.0, -0.0, -0.5, -1.0, -1.5, -2.0, -3.0, -4.0, -6.0])


def pack_weight(w, fmt):
    k, n = w.shape
    w = f64(np.asarray(w, np.float32).astype(ml_dtypes.bfloat16)).reshape(k // 32, 32, n)
    amax = np.abs(w).max(1)
    if fmt == "e4m3":
        byte = np.frexp(amax)[1] - 1 + 127 - 7
    else:
        mant, ex = np.frexp(amax / 6.0)
        byte = np.where(mant > 0.5, ex, ex - 1) + 127
    byte = np.clip(np.where(amax > 0, byte, 1), 1, 254)
    scaled = (w * np.exp2(127.0 - byte)[:, None, :]).reshape(k, n).astype(np.float32)
    by_word = np.ascontiguousarray(scaled.reshape(k // 512, 128, 4, n).transpose(0, 1, 3, 2))
    if fmt == "e4m3":
        words = by_word.astype(ml_dtypes.float8_e4m3fn).view(np.uint8)
    else:
        c = by_word.astype(ml_dtypes.float4_e2m1fn).view(np.uint8) & 0xF
        words = (c[..., 0::2] | (c[..., 1::2] << 4)).reshape(k // 512, 128, 2 * n)
    return np.ascontiguousarray(words), np.ascontiguousarray(byte.astype(np.uint8).reshape(k // 512, 16, n))


def unpack_weight(words, scales, fmt):
    g, _, n = scales.shape
    words = np.ascontiguousarray(words).reshape(g, 128, n, -1)
    if fmt == "e4m3":
        vals = words.view(ml_dtypes.float8_e4m3fn).astype(np.float64)
    else:
        nib = np.empty((g, 128, n, 4), np.uint8)
        nib[..., 0::2] = words & 0xF
        nib[..., 1::2] = words >> 4
        vals = E2M1[nib]
    vals = vals * np.repeat(np.exp2(scales.astype(np.float64) - 127.0), 8, axis=1)[..., None]
    return vals.transpose(0, 1, 3, 2).reshape(g * 512, n)


def pack_table(v):
    words, scales = pack_weight(v, "e4m3")
    return np.concatenate([words.reshape(words.shape[0], -1), scales.reshape(scales.shape[0], -1)], axis=1)


def unpack_table(tab):
    g, t = tab.shape[0], tab.shape[1] // 528
    return unpack_weight(tab[:, :512 * t].reshape(g, 128, t, 4), tab[:, 512 * t:].reshape(g, 16, t), "e4m3")


def silu(v):
    return v / (1.0 + np.exp(-np.maximum(v, -700.0)))


K, M, T, S = 2048, 512, 512, 256


def setup_inputs():
    n = np.random.standard_normal
    s = mx_kscale(K)[:, None]
    p_w4 = pack_weight(n((K, M)) / np.sqrt(K) / s, "e2m1")
    return {
        "tab": pack_table(n((K, T)) * s),
        "w4_words": p_w4[0],
        "w4_scales": p_w4[1],
        "w8": (n((K, M)) / np.sqrt(K) / s).astype(np.float32),
        "offs": striped(np.random.permutation(T)[:S]),
    }


def reference(tab, w4_words, w4_scales, w8, offs):
    tab_ = unpack_table(tab)[:, unstriped(offs)]
    w4_ = unpack_weight(w4_words, w4_scales, "e2m1")
    w8_ = mxq(f64(w8), 0, "e4m3")
    y = w4_.T @ tab_
    u = w8_.T @ tab_
    y = silu(y) * u
    return y

@@ -1,0 +1,154 @@
+from contextlib import ExitStack
+
+import concourse.mybir as mybir
+
+K, M, T, S = 2048, 512, 512, 256
+FLOPS = 2 * 2 * K * M * S
+
+F32 = mybir.dt.float32
+BF16 = mybir.dt.bfloat16
+I32 = mybir.dt.int32
+U32 = mybir.dt.uint32
+U16 = mybir.dt.uint16
+U8 = mybir.dt.uint8
+FP8X4 = mybir.dt.float8_e4m3fn_x4
+FP4X4 = mybir.dt.float4_e2m1fn_x4
+SILU = mybir.ActivationFunctionType.Silu
+MULT = mybir.AluOpType.mult
+
+P = 128
+PASSES = K // 512
+M_TILES = M // P
+WORD_BYTES = 512 * T
+
+
+def interleave(copy, grouped, raw, c0, c1):
+    copy(
+        out=grouped[:, c0:c1, :].rearrange("p (c i) t -> p c t i", i=4),
+        in_=raw[:, :, c0:c1].rearrange("p t (c i) -> p c t i", i=4),
+    )
+
+
+def tile_list_tabglu_none_kernel(tc, tab, w4_words, w4_scales, w8, offs, out):
+    nc = tc.nc
+    with ExitStack() as ctx:
+        held = ctx.enter_context(tc.tile_pool(name="held", bufs=1))
+        psum = ctx.enter_context(tc.psum_pool(name="psum", bufs=1))
+
+        offsets = held.tile([P, S // 16], U16, name="offsets")
+        tab_words = held.tile([P, PASSES, T], I32, name="tab_words", align_bytes=64)
+        tab_planes = held.tile([P, PASSES, T // 4], I32, name="tab_planes", align_bytes=64)
+        got_words = held.tile([P, PASSES, S], U32, name="got_words", align_bytes=64)
+        got_planes = held.tile([P, PASSES, S], U8, name="got_planes", align_bytes=64)
+        w4_codes = held.tile([P, PASSES, 2 * M], U8, name="w4_codes", align_bytes=64)
+        w4_planes = held.tile([P, PASSES, M // 4], I32, name="w4_planes", align_bytes=64)
+        raw = [held.tile([P, 4, M], F32, name=f"raw{a}", align_bytes=64) for a in range(PASSES)]
+        grouped = [held.tile([P, M, 4], BF16, name=f"grouped{a}", align_bytes=64) for a in range(PASSES)]
+        w8_codes = held.tile([P, PASSES, M], U32, name="w8_codes", align_bytes=64)
+        w8_planes = held.tile([P, PASSES, M], U8, name="w8_planes", align_bytes=64)
+        gate = [held.tile([P, S], F32, name=f"gate{m}") for m in range(M_TILES)]
+        result = [held.tile([P, S], F32, name=f"result{m}") for m in range(M_TILES)]
+        warm = held.tile([P, 1], F32, name="warm")
+        e_sum = [psum.tile([P, S], F32, name=f"e_sum{m}") for m in range(M_TILES)]
+        u_sum = [psum.tile([P, S], F32, name=f"u_sum{m}") for m in range(M_TILES)]
+
+        nc.vector.memset(tab_planes[:], 0)
+        nc.gpsimd.memset(w4_planes[:], 0)
+        nc.gpsimd.memset(warm[:], 0.0)
+
+        nc.sync.dma_start(offsets[:], offs)
+        for a in range(0, PASSES, 2):
+            nc.sync.dma_start(
+                out=tab_words[:, a : a + 2, :],
+                in_=tab[a : a + 2, 0:WORD_BYTES].rearrange("a (p b) -> p a b", p=P).bitcast(I32),
+            )
+        for q in range(4):
+            base = WORD_BYTES + 4 * q * T
+            nc.scalar.dma_start(
+                out=tab_planes[32 * q : 32 * q + 4, :, :],
+                in_=tab[:, base : base + 4 * T].rearrange("a (r t) -> r a t", r=4).bitcast(I32),
+            )
+        nc.scalar.activation(warm[:], warm[:], SILU)
+        nc.sync.dma_start(out=raw[0][:], in_=w8[0:512, :].rearrange("(p j) n -> p j n", j=4))
+        for q in range(4):
+            nc.scalar.dma_start(
+                out=w4_planes[32 * q : 32 * q + 4, :, :],
+                in_=w4_scales[:, 4 * q : 4 * q + 4, :].rearrange("a r n -> r a n").bitcast(I32),
+            )
+        nc.sync.dma_start(out=w4_codes[:].bitcast(I32), in_=w4_words.rearrange("a p b -> p a b").bitcast(I32))
+        for a in range(1, PASSES - 1):
+            nc.sync.dma_start(out=raw[a][:], in_=w8[512 * a : 512 * a + 512, :].rearrange("(p j) n -> p j n", j=4))
+        last = PASSES - 1
+        for c0 in range(0, M, 256):
+            nc.sync.dma_start(
+                out=raw[last][:, :, c0 : c0 + 256],
+                in_=w8[512 * last :, c0 : c0 + 256].rearrange("(p j) n -> p j n", j=4),
+            )
+
+        for a in range(PASSES):
+            nc.vector.tensor_copy(got_words[:, a, :], tab_words[:, a, :].bitcast(U32).indirect(offsets[:]))
+        for a in range(PASSES):
+            nc.vector.tensor_copy(got_planes[:, a, :], tab_planes[:, a, :].bitcast(U8).indirect(offsets[:]))
+
+        def quantize(a, c0, c1):
+            nc.vector.quantize_mx(
+                out=w8_codes[:, a, c0:c1].bitcast(FP8X4),
+                scales=w8_planes[:, a, c0:c1],
+                in_=grouped[a][:, c0:c1, :].rearrange("p c t -> p (c t)"),
+            )
+
+        def multiply_u(a, m):
+            cols = slice(P * m, P * m + P)
+            nc.tensor.matmul_mx(
+                out=u_sum[m][:],
+                lhsT=w8_codes[:, a, cols].bitcast(FP8X4),
+                lhsT_scale=w8_planes[:, a, cols],
+                rhs=got_words[:, a, :].bitcast(FP8X4),
+                rhs_scale=got_planes[:, a, :],
+                start=(a == 0),
+                stop=(a == last),
+            )
+
+        def multiply_e(m):
+            for h in range(0, S, P):
+                for a in range(PASSES):
+                    nc.tensor.matmul_mx(
+                        out=e_sum[m][:, h : h + P],
+                        lhsT=w4_codes[:, a, 2 * P * m : 2 * P * m + 2 * P].bitcast(FP4X4),
+                        lhsT_scale=w4_planes[:, a, 32 * m : 32 * m + 32].bitcast(U8),
+                        rhs=got_words[:, a, h : h + P].bitcast(FP8X4),
+                        rhs_scale=got_planes[:, a, h : h + P],
+                        start=(a == 0),
+                        stop=(a == last),
+                    )
+
+        interleave(nc.scalar.copy, grouped[0], raw[0], 0, 256)
+        interleave(nc.scalar.copy, grouped[0], raw[0], 256, 512)
+        quantize(0, 0, 512)
+        for m in range(M_TILES):
+            multiply_e(m)
+        for m in range(M_TILES):
+            multiply_u(0, m)
+
+        for a in range(1, last):
+            interleave(nc.vector.tensor_copy, grouped[a], raw[a], 0, 256)
+            interleave(nc.scalar.copy, grouped[a], raw[a], 256, 512)
+            quantize(a, 0, 256)
+            quantize(a, 256, 512)
+            for m in range(M_TILES):
+                multiply_u(a, m)
+            if a == 1:
+                for m in range(M_TILES):
+                    nc.scalar.activation(gate[m][:], e_sum[m][:], SILU)
+
+        for c0 in range(0, M, 256):
+            interleave(nc.vector.tensor_copy, grouped[last], raw[last], c0, c0 + 128)
+            interleave(nc.scalar.copy, grouped[last], raw[last], c0 + 128, c0 + 256)
+            for b in (c0, c0 + P):
+                m = b // P
+                quantize(last, b, b + P)
+                multiply_u(last, m)
+            for b in (c0, c0 + P):
+                m = b // P
+                nc.vector.tensor_tensor(out=result[m][:], in0=u_sum[m][:], in1=gate[m][:], op=MULT)
+                nc.sync.dma_start(out=out[P * m : P * m + P, :], in_=result[m][:])

@@ -56,12 +56,20 @@ def tile_list_tabglu_none_kernel(tc, tab, w4_words, w4_scales, w8, offs, out):
         nc.gpsimd.memset(w4_planes[:], 0)
         nc.gpsimd.memset(warm[:], 0.0)
 
-        nc.sync.dma_start(offsets[:], offs)
-        for a in range(0, PASSES, 2):
+        def load_tab(a, b):
             nc.sync.dma_start(
-                out=tab_words[:, a : a + 2, :],
-                in_=tab[a : a + 2, 0:WORD_BYTES].rearrange("a (p b) -> p a b", p=P).bitcast(I32),
+                out=tab_words[:, a:b, :],
+                in_=tab[a:b, 0:WORD_BYTES].rearrange("a (p b) -> p a b", p=P).bitcast(I32),
             )
+
+        def load_w8(a, c0, c1):
+            nc.sync.dma_start(
+                out=raw[a][:, :, c0:c1],
+                in_=w8[512 * a : 512 * a + 512, c0:c1].rearrange("(p j) n -> p j n", j=4),
+            )
+
+        load_tab(0, 1)
+        nc.sync.dma_start(offsets[:], offs)
         for q in range(4):
             base = WORD_BYTES + 4 * q * T
             nc.scalar.dma_start(
@@ -69,26 +77,31 @@ def tile_list_tabglu_none_kernel(tc, tab, w4_words, w4_scales, w8, offs, out):
                 in_=tab[:, base : base + 4 * T].rearrange("a (r t) -> r a t", r=4).bitcast(I32),
             )
         nc.scalar.activation(warm[:], warm[:], SILU)
-        nc.sync.dma_start(out=raw[0][:], in_=w8[0:512, :].rearrange("(p j) n -> p j n", j=4))
+        load_w8(0, 0, M)
+        load_tab(1, PASSES)
         for q in range(4):
-            nc.scalar.dma_start(
+            nc.gpsimd.dma_start(
                 out=w4_planes[32 * q : 32 * q + 4, :, :],
                 in_=w4_scales[:, 4 * q : 4 * q + 4, :].rearrange("a r n -> r a n").bitcast(I32),
             )
         nc.sync.dma_start(out=w4_codes[:].bitcast(I32), in_=w4_words.rearrange("a p b -> p a b").bitcast(I32))
-        for a in range(1, PASSES - 1):
-            nc.sync.dma_start(out=raw[a][:], in_=w8[512 * a : 512 * a + 512, :].rearrange("(p j) n -> p j n", j=4))
+        load_w8(1, 0, M)
+        for c0 in (0, 256):
+            for a in (2, 3):
+                load_w8(a, c0, c0 + 256)
         last = PASSES - 1
-        for c0 in range(0, M, 256):
-            nc.sync.dma_start(
-                out=raw[last][:, :, c0 : c0 + 256],
-                in_=w8[512 * last :, c0 : c0 + 256].rearrange("(p j) n -> p j n", j=4),
-            )
 
-        for a in range(PASSES):
+        def gather_words(a):
             nc.vector.tensor_copy(got_words[:, a, :], tab_words[:, a, :].bitcast(U32).indirect(offsets[:]))
-        for a in range(PASSES):
+
+        def gather_planes(a):
             nc.vector.tensor_copy(got_planes[:, a, :], tab_planes[:, a, :].bitcast(U8).indirect(offsets[:]))
+
+        gather_words(0)
+        for a in range(PASSES):
+            gather_planes(a)
+        for a in range(1, PASSES):
+            gather_words(a)
 
         def quantize(a, c0, c1):
             nc.vector.quantize_mx(
@@ -122,33 +135,60 @@ def tile_list_tabglu_none_kernel(tc, tab, w4_words, w4_scales, w8, offs, out):
                         stop=(a == last),
                     )
 
-        interleave(nc.scalar.copy, grouped[0], raw[0], 0, 256)
-        interleave(nc.scalar.copy, grouped[0], raw[0], 256, 512)
+        def vector_copy(a, c0, c1):
+            interleave(nc.vector.tensor_copy, grouped[a], raw[a], c0, c1)
+
+        def scalar_copy(a, c0, c1):
+            interleave(nc.scalar.copy, grouped[a], raw[a], c0, c1)
+
+        def silu(m):
+            nc.scalar.activation(gate[m][:], e_sum[m][:], SILU)
+
+        def finish(m):
+            nc.vector.tensor_tensor(out=result[m][:], in0=u_sum[m][:], in1=gate[m][:], op=MULT)
+            nc.sync.dma_start(out=out[P * m : P * m + P, :], in_=result[m][:])
+
+        scalar_copy(0, 0, 256)
+        scalar_copy(0, 256, 512)
         quantize(0, 0, 512)
         for m in range(M_TILES):
             multiply_e(m)
         for m in range(M_TILES):
             multiply_u(0, m)
 
-        for a in range(1, last):
-            interleave(nc.vector.tensor_copy, grouped[a], raw[a], 0, 256)
-            interleave(nc.scalar.copy, grouped[a], raw[a], 256, 512)
-            quantize(a, 0, 256)
-            quantize(a, 256, 512)
-            for m in range(M_TILES):
-                multiply_u(a, m)
-            if a == 1:
-                for m in range(M_TILES):
-                    nc.scalar.activation(gate[m][:], e_sum[m][:], SILU)
+        vector_copy(1, 0, 256)
+        scalar_copy(1, 256, 512)
+        quantize(1, 0, 256)
+        quantize(1, 256, 512)
+        for m in range(M_TILES):
+            multiply_u(1, m)
 
-        for c0 in range(0, M, 256):
-            interleave(nc.vector.tensor_copy, grouped[last], raw[last], c0, c0 + 128)
-            interleave(nc.scalar.copy, grouped[last], raw[last], c0 + 128, c0 + 256)
-            for b in (c0, c0 + P):
-                m = b // P
-                quantize(last, b, b + P)
-                multiply_u(last, m)
-            for b in (c0, c0 + P):
-                m = b // P
-                nc.vector.tensor_tensor(out=result[m][:], in0=u_sum[m][:], in1=gate[m][:], op=MULT)
-                nc.sync.dma_start(out=out[P * m : P * m + P, :], in_=result[m][:])
+        vector_copy(2, 0, 128)
+        scalar_copy(2, 128, 256)
+        quantize(2, 0, 256)
+        multiply_u(2, 0)
+        multiply_u(2, 1)
+        silu(0)
+        silu(1)
+        vector_copy(3, 0, 128)
+        scalar_copy(3, 128, 256)
+        quantize(3, 0, 256)
+        multiply_u(3, 0)
+        multiply_u(3, 1)
+        silu(2)
+        vector_copy(2, 256, 384)
+        scalar_copy(2, 384, 512)
+        finish(0)
+        quantize(2, 256, 512)
+        multiply_u(2, 2)
+        multiply_u(2, 3)
+        silu(3)
+        finish(1)
+        vector_copy(3, 256, 384)
+        scalar_copy(3, 384, 512)
+        quantize(3, 256, 384)
+        multiply_u(3, 2)
+        quantize(3, 384, 512)
+        multiply_u(3, 3)
+        finish(2)
+        finish(3)

@@ -72,23 +72,23 @@ def tile_list_tabglu_none_kernel(tc, tab, w4_words, w4_scales, w8, offs, out):
         nc.sync.dma_start(offsets[:], offs)
         for q in range(4):
             base = WORD_BYTES + 4 * q * T
-            nc.scalar.dma_start(
+            nc.sync.dma_start(
                 out=tab_planes[32 * q : 32 * q + 4, :, :],
                 in_=tab[:, base : base + 4 * T].rearrange("a (r t) -> r a t", r=4).bitcast(I32),
             )
         nc.scalar.activation(warm[:], warm[:], SILU)
-        load_w8(0, 0, M)
+        nc.sync.dma_start(out=w4_codes[:].bitcast(I32), in_=w4_words.rearrange("a p b -> p a b").bitcast(I32))
         load_tab(1, PASSES)
         for q in range(4):
-            nc.gpsimd.dma_start(
+            nc.sync.dma_start(
                 out=w4_planes[32 * q : 32 * q + 4, :, :],
                 in_=w4_scales[:, 4 * q : 4 * q + 4, :].rearrange("a r n -> r a n").bitcast(I32),
             )
-        nc.sync.dma_start(out=w4_codes[:].bitcast(I32), in_=w4_words.rearrange("a p b -> p a b").bitcast(I32))
+        load_w8(0, 0, M)
         load_w8(1, 0, M)
-        for c0 in (0, 256):
-            for a in (2, 3):
-                load_w8(a, c0, c0 + 256)
+        load_w8(2, 0, M)
+        load_w8(3, 0, 256)
+        load_w8(3, 256, M)
         last = PASSES - 1
 
         def gather_words(a):
@@ -122,18 +122,16 @@ def tile_list_tabglu_none_kernel(tc, tab, w4_words, w4_scales, w8, offs, out):
                 stop=(a == last),
             )
 
-        def multiply_e(m):
-            for h in range(0, S, P):
-                for a in range(PASSES):
-                    nc.tensor.matmul_mx(
-                        out=e_sum[m][:, h : h + P],
-                        lhsT=w4_codes[:, a, 2 * P * m : 2 * P * m + 2 * P].bitcast(FP4X4),
-                        lhsT_scale=w4_planes[:, a, 32 * m : 32 * m + 32].bitcast(U8),
-                        rhs=got_words[:, a, h : h + P].bitcast(FP8X4),
-                        rhs_scale=got_planes[:, a, h : h + P],
-                        start=(a == 0),
-                        stop=(a == last),
-                    )
+        def multiply_e(a, m, h):
+            nc.tensor.matmul_mx(
+                out=e_sum[m][:, h : h + P],
+                lhsT=w4_codes[:, a, 2 * P * m : 2 * P * m + 2 * P].bitcast(FP4X4),
+                lhsT_scale=w4_planes[:, a, 32 * m : 32 * m + 32].bitcast(U8),
+                rhs=got_words[:, a, h : h + P].bitcast(FP8X4),
+                rhs_scale=got_planes[:, a, h : h + P],
+                start=(a == 0),
+                stop=(a == last),
+            )
 
         def vector_copy(a, c0, c1):
             interleave(nc.vector.tensor_copy, grouped[a], raw[a], c0, c1)
@@ -148,47 +146,52 @@ def tile_list_tabglu_none_kernel(tc, tab, w4_words, w4_scales, w8, offs, out):
             nc.vector.tensor_tensor(out=result[m][:], in0=u_sum[m][:], in1=gate[m][:], op=MULT)
             nc.sync.dma_start(out=out[P * m : P * m + P, :], in_=result[m][:])
 
-        scalar_copy(0, 0, 256)
-        scalar_copy(0, 256, 512)
+        for a in range(PASSES):
+            for m in range(M_TILES):
+                multiply_e(a, m, 0)
+        for m in range(M_TILES):
+            for a in range(PASSES):
+                multiply_e(a, m, P)
+        vector_copy(0, 0, 192)
+        scalar_copy(0, 192, 512)
         quantize(0, 0, 512)
-        for m in range(M_TILES):
-            multiply_e(m)
-        for m in range(M_TILES):
-            multiply_u(0, m)
-
-        vector_copy(1, 0, 256)
-        scalar_copy(1, 256, 512)
-        quantize(1, 0, 256)
-        quantize(1, 256, 512)
-        for m in range(M_TILES):
-            multiply_u(1, m)
-
-        vector_copy(2, 0, 128)
-        scalar_copy(2, 128, 256)
+        multiply_u(0, 0)
+        multiply_u(0, 1)
+        multiply_u(0, 2)
+        multiply_u(0, 3)
+        vector_copy(1, 0, 192)
+        scalar_copy(1, 192, 512)
+        quantize(1, 0, 512)
+        multiply_u(1, 0)
+        multiply_u(1, 1)
+        multiply_u(1, 2)
+        multiply_u(1, 3)
+        silu(0)
+        vector_copy(2, 0, 192)
+        scalar_copy(2, 192, 256)
         quantize(2, 0, 256)
+        scalar_copy(2, 256, 512)
+        quantize(2, 256, 512)
         multiply_u(2, 0)
         multiply_u(2, 1)
-        silu(0)
+        multiply_u(2, 2)
+        multiply_u(2, 3)
         silu(1)
         vector_copy(3, 0, 128)
         scalar_copy(3, 128, 256)
-        quantize(3, 0, 256)
+        quantize(3, 0, 128)
         multiply_u(3, 0)
+        quantize(3, 128, 256)
         multiply_u(3, 1)
-        silu(2)
-        vector_copy(2, 256, 384)
-        scalar_copy(2, 384, 512)
-        finish(0)
-        quantize(2, 256, 512)
-        multiply_u(2, 2)
-        multiply_u(2, 3)
-        silu(3)
-        finish(1)
         vector_copy(3, 256, 384)
         scalar_copy(3, 384, 512)
+        silu(2)
+        silu(3)
         quantize(3, 256, 384)
         multiply_u(3, 2)
         quantize(3, 384, 512)
         multiply_u(3, 3)
+        finish(0)
+        finish(1)
         finish(2)
         finish(3)

@@ -34,6 +34,7 @@ def tile_list_tabglu_none_kernel(tc, tab, w4_words, w4_scales, w8, offs, out):
     with ExitStack() as ctx:
         held = ctx.enter_context(tc.tile_pool(name="held", bufs=1))
         psum = ctx.enter_context(tc.psum_pool(name="psum", bufs=1))
+        gate_psum = ctx.enter_context(tc.psum_pool(name="gate_psum", bufs=3))
 
         offsets = held.tile([P, S // 16], U16, name="offsets")
         tab_words = held.tile([P, PASSES, T], I32, name="tab_words", align_bytes=64)
@@ -49,12 +50,11 @@ def tile_list_tabglu_none_kernel(tc, tab, w4_words, w4_scales, w8, offs, out):
         gate = [held.tile([P, S], F32, name=f"gate{m}") for m in range(M_TILES)]
         result = [held.tile([P, S], F32, name=f"result{m}") for m in range(M_TILES)]
         warm = held.tile([P, 1], F32, name="warm")
-        e_sum = [psum.tile([P, S], F32, name=f"e_sum{m}") for m in range(M_TILES)]
         u_sum = [psum.tile([P, S], F32, name=f"u_sum{m}") for m in range(M_TILES)]
 
-        nc.vector.memset(tab_planes[:], 0)
-        nc.gpsimd.memset(w4_planes[:], 0)
+        nc.gpsimd.memset(tab_planes[:], 0)
         nc.gpsimd.memset(warm[:], 0.0)
+        nc.vector.memset(w4_planes[:], 0)
 
         def load_tab(a, b):
             nc.sync.dma_start(
@@ -70,19 +70,18 @@ def tile_list_tabglu_none_kernel(tc, tab, w4_words, w4_scales, w8, offs, out):
 
         load_tab(0, 1)
         nc.sync.dma_start(offsets[:], offs)
-        for q in range(4):
-            base = WORD_BYTES + 4 * q * T
+        for r in range(4):
             nc.sync.dma_start(
-                out=tab_planes[32 * q : 32 * q + 4, :, :],
-                in_=tab[:, base : base + 4 * T].rearrange("a (r t) -> r a t", r=4).bitcast(I32),
+                out=tab_planes[r:P:32, :, :],
+                in_=tab[:, WORD_BYTES:].rearrange("a (q r t) -> r q a t", q=4, r=4)[r].bitcast(I32),
             )
         nc.scalar.activation(warm[:], warm[:], SILU)
         nc.sync.dma_start(out=w4_codes[:].bitcast(I32), in_=w4_words.rearrange("a p b -> p a b").bitcast(I32))
         load_tab(1, PASSES)
-        for q in range(4):
+        for r in range(4):
             nc.sync.dma_start(
-                out=w4_planes[32 * q : 32 * q + 4, :, :],
-                in_=w4_scales[:, 4 * q : 4 * q + 4, :].rearrange("a r n -> r a n").bitcast(I32),
+                out=w4_planes[r:P:32, :, :],
+                in_=w4_scales.rearrange("a (q r) n -> r q a n", r=4)[r].bitcast(I32),
             )
         load_w8(0, 0, M)
         load_w8(1, 0, M)
@@ -133,6 +132,8 @@ def tile_list_tabglu_none_kernel(tc, tab, w4_words, w4_scales, w8, offs, out):
                 stop=(a == last),
             )
 
+        e_sum = [gate_psum.tile([P, S], F32, name="e_sum") for m in range(3)]
+
         def vector_copy(a, c0, c1):
             interleave(nc.vector.tensor_copy, grouped[a], raw[a], c0, c1)
 
@@ -147,46 +148,49 @@ def tile_list_tabglu_none_kernel(tc, tab, w4_words, w4_scales, w8, offs, out):
             nc.sync.dma_start(out=out[P * m : P * m + P, :], in_=result[m][:])
 
         for a in range(PASSES):
-            for m in range(M_TILES):
+            for m in range(3):
                 multiply_e(a, m, 0)
-        for m in range(M_TILES):
+        for m in range(3):
             for a in range(PASSES):
                 multiply_e(a, m, P)
-        vector_copy(0, 0, 192)
-        scalar_copy(0, 192, 512)
+        vector_copy(0, 0, 320)
+        scalar_copy(0, 320, 512)
         quantize(0, 0, 512)
         multiply_u(0, 0)
         multiply_u(0, 1)
         multiply_u(0, 2)
         multiply_u(0, 3)
-        vector_copy(1, 0, 192)
-        scalar_copy(1, 192, 512)
+        vector_copy(1, 0, 320)
+        scalar_copy(1, 320, 512)
         quantize(1, 0, 512)
         multiply_u(1, 0)
         multiply_u(1, 1)
         multiply_u(1, 2)
         multiply_u(1, 3)
         silu(0)
-        vector_copy(2, 0, 192)
-        scalar_copy(2, 192, 256)
-        quantize(2, 0, 256)
+        e_sum.append(gate_psum.tile([P, S], F32, name="e_sum"))
+        for h in (0, P):
+            for a in range(PASSES):
+                multiply_e(a, 3, h)
+        silu(1)
+        silu(2)
+        vector_copy(2, 0, 256)
         scalar_copy(2, 256, 512)
+        quantize(2, 0, 256)
         quantize(2, 256, 512)
         multiply_u(2, 0)
         multiply_u(2, 1)
         multiply_u(2, 2)
         multiply_u(2, 3)
-        silu(1)
-        vector_copy(3, 0, 128)
+        scalar_copy(3, 0, 128)
         scalar_copy(3, 128, 256)
         quantize(3, 0, 128)
         multiply_u(3, 0)
+        vector_copy(3, 256, 416)
+        scalar_copy(3, 416, 512)
+        silu(3)
         quantize(3, 128, 256)
         multiply_u(3, 1)
-        vector_copy(3, 256, 384)
-        scalar_copy(3, 384, 512)
-        silu(2)
-        silu(3)
         quantize(3, 256, 384)
         multiply_u(3, 2)
         quantize(3, 384, 512)

from contextlib import ExitStack

import concourse.mybir as mybir

K, M, T, S = 2048, 512, 512, 256
FLOPS = 2 * 2 * K * M * S

F32 = mybir.dt.float32
BF16 = mybir.dt.bfloat16
I32 = mybir.dt.int32
U32 = mybir.dt.uint32
U16 = mybir.dt.uint16
U8 = mybir.dt.uint8
FP8X4 = mybir.dt.float8_e4m3fn_x4
FP4X4 = mybir.dt.float4_e2m1fn_x4
SILU = mybir.ActivationFunctionType.Silu
MULT = mybir.AluOpType.mult

P = 128
PASSES = K // 512
M_TILES = M // P
WORD_BYTES = 512 * T


def interleave(copy, grouped, raw, c0, c1):
    copy(
        out=grouped[:, c0:c1, :].rearrange("p (c i) t -> p c t i", i=4),
        in_=raw[:, :, c0:c1].rearrange("p t (c i) -> p c t i", i=4),
    )


def tile_list_tabglu_none_kernel(tc, tab, w4_words, w4_scales, w8, offs, out):
    nc = tc.nc
    with ExitStack() as ctx:
        held = ctx.enter_context(tc.tile_pool(name="held", bufs=1))
        psum = ctx.enter_context(tc.psum_pool(name="psum", bufs=1))
        gate_psum = ctx.enter_context(tc.psum_pool(name="gate_psum", bufs=3))

        offsets = held.tile([P, S // 16], U16, name="offsets")
        tab_words = held.tile([P, PASSES, T], I32, name="tab_words", align_bytes=64)
        tab_planes = held.tile([P, PASSES, T // 4], I32, name="tab_planes", align_bytes=64)
        got_words = held.tile([P, PASSES, S], U32, name="got_words", align_bytes=64)
        got_planes = held.tile([P, PASSES, S], U8, name="got_planes", align_bytes=64)
        w4_codes = held.tile([P, PASSES, 2 * M], U8, name="w4_codes", align_bytes=64)
        w4_planes = held.tile([P, PASSES, M // 4], I32, name="w4_planes", align_bytes=64)
        raw = [held.tile([P, 4, M], F32, name=f"raw{a}", align_bytes=64) for a in range(PASSES)]
        grouped = [held.tile([P, M, 4], BF16, name=f"grouped{a}", align_bytes=64) for a in range(PASSES)]
        w8_codes = held.tile([P, PASSES, M], U32, name="w8_codes", align_bytes=64)
        w8_planes = held.tile([P, PASSES, M], U8, name="w8_planes", align_bytes=64)
        gate = [held.tile([P, S], F32, name=f"gate{m}") for m in range(M_TILES)]
        result = [held.tile([P, S], F32, name=f"result{m}") for m in range(M_TILES)]
        warm = held.tile([P, 1], F32, name="warm")
        u_sum = [psum.tile([P, S], F32, name=f"u_sum{m}") for m in range(M_TILES)]

        nc.gpsimd.memset(tab_planes[:], 0)
        nc.gpsimd.memset(warm[:], 0.0)
        nc.vector.memset(w4_planes[:], 0)

        def load_tab(a, b):
            nc.sync.dma_start(
                out=tab_words[:, a:b, :],
                in_=tab[a:b, 0:WORD_BYTES].rearrange("a (p b) -> p a b", p=P).bitcast(I32),
            )

        def load_w8(a, c0, c1):
            nc.sync.dma_start(
                out=raw[a][:, :, c0:c1],
                in_=w8[512 * a : 512 * a + 512, c0:c1].rearrange("(p j) n -> p j n", j=4),
            )

        load_tab(0, 1)
        nc.sync.dma_start(offsets[:], offs)
        for r in range(4):
            nc.sync.dma_start(
                out=tab_planes[r:P:32, :, :],
                in_=tab[:, WORD_BYTES:].rearrange("a (q r t) -> r q a t", q=4, r=4)[r].bitcast(I32),
            )
        nc.scalar.activation(warm[:], warm[:], SILU)
        nc.sync.dma_start(out=w4_codes[:].bitcast(I32), in_=w4_words.rearrange("a p b -> p a b").bitcast(I32))
        load_tab(1, PASSES)
        for r in range(4):
            nc.sync.dma_start(
                out=w4_planes[r:P:32, :, :],
                in_=w4_scales.rearrange("a (q r) n -> r q a n", r=4)[r].bitcast(I32),
            )
        load_w8(0, 0, M)
        load_w8(1, 0, M)
        load_w8(2, 0, M)
        load_w8(3, 0, 256)
        load_w8(3, 256, M)
        last = PASSES - 1

        def gather_words(a):
            nc.vector.tensor_copy(got_words[:, a, :], tab_words[:, a, :].bitcast(U32).indirect(offsets[:]))

        def gather_planes(a):
            nc.vector.tensor_copy(got_planes[:, a, :], tab_planes[:, a, :].bitcast(U8).indirect(offsets[:]))

        gather_words(0)
        for a in range(PASSES):
            gather_planes(a)
        for a in range(1, PASSES):
            gather_words(a)

        def quantize(a, c0, c1):
            nc.vector.quantize_mx(
                out=w8_codes[:, a, c0:c1].bitcast(FP8X4),
                scales=w8_planes[:, a, c0:c1],
                in_=grouped[a][:, c0:c1, :].rearrange("p c t -> p (c t)"),
            )

        def multiply_u(a, m):
            cols = slice(P * m, P * m + P)
            nc.tensor.matmul_mx(
                out=u_sum[m][:],
                lhsT=w8_codes[:, a, cols].bitcast(FP8X4),
                lhsT_scale=w8_planes[:, a, cols],
                rhs=got_words[:, a, :].bitcast(FP8X4),
                rhs_scale=got_planes[:, a, :],
                start=(a == 0),
                stop=(a == last),
            )

        def multiply_e(a, m, h):
            nc.tensor.matmul_mx(
                out=e_sum[m][:, h : h + P],
                lhsT=w4_codes[:, a, 2 * P * m : 2 * P * m + 2 * P].bitcast(FP4X4),
                lhsT_scale=w4_planes[:, a, 32 * m : 32 * m + 32].bitcast(U8),
                rhs=got_words[:, a, h : h + P].bitcast(FP8X4),
                rhs_scale=got_planes[:, a, h : h + P],
                start=(a == 0),
                stop=(a == last),
            )

        e_sum = [gate_psum.tile([P, S], F32, name="e_sum") for m in range(3)]

        def vector_copy(a, c0, c1):
            interleave(nc.vector.tensor_copy, grouped[a], raw[a], c0, c1)

        def scalar_copy(a, c0, c1):
            interleave(nc.scalar.copy, grouped[a], raw[a], c0, c1)

        def silu(m):
            nc.scalar.activation(gate[m][:], e_sum[m][:], SILU)

        def finish(m):
            nc.vector.tensor_tensor(out=result[m][:], in0=u_sum[m][:], in1=gate[m][:], op=MULT)
            nc.sync.dma_start(out=out[P * m : P * m + P, :], in_=result[m][:])

        for a in range(PASSES):
            for m in range(3):
                multiply_e(a, m, 0)
        for m in range(3):
            for a in range(PASSES):
                multiply_e(a, m, P)
        vector_copy(0, 0, 320)
        scalar_copy(0, 320, 512)
        quantize(0, 0, 512)
        multiply_u(0, 0)
        multiply_u(0, 1)
        multiply_u(0, 2)
        multiply_u(0, 3)
        vector_copy(1, 0, 320)
        scalar_copy(1, 320, 512)
        quantize(1, 0, 512)
        multiply_u(1, 0)
        multiply_u(1, 1)
        multiply_u(1, 2)
        multiply_u(1, 3)
        silu(0)
        e_sum.append(gate_psum.tile([P, S], F32, name="e_sum"))
        for h in (0, P):
            for a in range(PASSES):
                multiply_e(a, 3, h)
        silu(1)
        silu(2)
        vector_copy(2, 0, 256)
        scalar_copy(2, 256, 512)
        quantize(2, 0, 256)
        quantize(2, 256, 512)
        multiply_u(2, 0)
        multiply_u(2, 1)
        multiply_u(2, 2)
        multiply_u(2, 3)
        scalar_copy(3, 0, 128)
        scalar_copy(3, 128, 256)
        quantize(3, 0, 128)
        multiply_u(3, 0)
        vector_copy(3, 256, 416)
        scalar_copy(3, 416, 512)
        silu(3)
        quantize(3, 128, 256)
        multiply_u(3, 1)
        quantize(3, 256, 384)
        multiply_u(3, 2)
        quantize(3, 384, 512)
        multiply_u(3, 3)
        finish(0)
        finish(1)
        finish(2)
        finish(3)
